import numpy as np
CORES = [128,136,144,152,160,168,176,184,192,200,208,216,224,232,240,248,384,392,400,408,416,424,432,440,448,456,464,472,480,488,496,504]
N = 32
def setup_inputs(rng):
    return {"x": rng.standard_normal((N, 128, 512), dtype=np.float32)}
def reference(x):
    b = 512 // N
    blocks = x.reshape(N, 128, N, b)
    return {"y": np.ascontiguousarray(blocks.transpose(2, 1, 0, 3)).reshape(N, 128, 512)}

@@ -1,0 +1,89 @@
+import comms_topo
+from concourse.bass import DstId, RemoteDMATransfer
+
+B = 16
+
+SCRATCH = {
+    "send": ("sbuf", [128, 512], "float32"),
+    "land": ("sbuf", [128, 512], "float32"),
+}
+SEMAPHORES = ["loaded", "kept", "read", "arrived", "stored"]
+
+MATE_PORT_CORE = (6, 6, 7, 7, 2, 2, 3, 3)
+SAME_PARITY_CORE = (None, 1, 4, 4, 4, 5, 5, 5)
+
+
+def relay_of(src, dst):
+    hs, hd = comms_topo.host(src), comms_topo.host(dst)
+    c, cd = comms_topo.chip(src), comms_topo.chip(dst)
+    t = (cd // 2 - c // 2) % 8
+    same_parity = c % 2 == cd % 2
+    if hs == hd:
+        return hs * 128 + c * 8 + (SAME_PARITY_CORE[t] if same_parity else MATE_PORT_CORE[t])
+    if same_parity:
+        return (hs ^ 1) * 128 + cd * 8 + t
+    return (3 - hs) * 128 + c * 8 + MATE_PORT_CORE[t]
+
+
+def jobs_of(relay, cores):
+    return [(i, j) for i, s in enumerate(cores) for j, d in enumerate(cores) if s != d and relay_of(s, d) == relay]
+
+
+def engines_each(n):
+    return {1: 8, 2: 4, 3: 2}[n]
+
+
+def block(t, k):
+    return t[:, k * B:(k + 1) * B]
+
+
+def transfer(T, src_core, dst_core, src_ap, dst_ap, mask):
+    rid, pid = comms_topo.addr(dst_core, src_core)
+    return RemoteDMATransfer(dst_ids=[DstId(rid=rid, pnc=pid)], dma_engine_mask=mask, remote_sem=T.sem.arrived,
+                             src=src_ap, dst=dst_ap)
+
+
+def rank_program(g, core, T, topo):
+    cores = list(T.cores)
+    rank = T.rank_of(core)
+
+    if rank is None:
+        jobs = jobs_of(core, cores)
+        if not jobs:
+            return
+        e = engines_each(len(jobs))
+        g.wait_ge(T.sem.arrived, len(jobs))
+        g.remote_dma_fused(
+            [transfer(T, core, cores[j], block(T.land, slot), block(T.land, i), ((1 << e) - 1) << (slot * e))
+             for slot, (i, j) in enumerate(jobs)],
+            local_sem=T.sem.read)
+        g.wait_ge(T.sem.read, e * len(jobs))
+        return
+
+    g.dma_start(T.send[:], T.x[:]).then_inc(T.sem.loaded, 16)
+    g.dma_start(block(T.land, rank), block(T.x, rank)).then_inc(T.sem.kept, 16)
+
+    off_chip, on_chip, expected = [], [], 0
+    for j, d in enumerate(cores):
+        if d == core:
+            continue
+        out_relay = relay_of(core, d)
+        slot = jobs_of(out_relay, cores).index((rank, j))
+        (on_chip if out_relay // 8 == core // 8 else off_chip).append((out_relay, j, slot))
+        expected += engines_each(len(jobs_of(relay_of(d, core), cores)))
+    off_chip.sort(key=lambda w: comms_topo.rack(comms_topo.host(w[0])) == comms_topo.rack(comms_topo.host(core)))
+
+    g.wait_ge(T.sem.loaded, 16)
+    for k in range(2):
+        g.remote_dma_fused(
+            [transfer(T, core, r, block(T.send, j), block(T.land, slot), 1 << n)
+             for n, (r, j, slot) in enumerate(off_chip[8 * k:8 * k + 8])] +
+            [transfer(T, core, r, block(T.send, j), block(T.land, slot), 1 << (8 + n))
+             for n, (r, j, slot) in enumerate(on_chip[8 * k:8 * k + 8])],
+            local_sem=T.sem.read)
+
+    g.wait_ge(T.sem.arrived, expected)
+    g.wait_ge(T.sem.kept, 16)
+    g.dma_start(T.y[:], T.land[:]).then_inc(T.sem.stored, 16)
+    g.wait_ge(T.sem.read, len(off_chip) + len(on_chip))
+    g.wait_ge(T.sem.stored, 16)

@@ -11,6 +11,7 @@ SEMAPHORES = ["loaded", "kept", "read", "arrived", "stored"]
 
 MATE_PORT_CORE = (6, 6, 7, 7, 2, 2, 3, 3)
 SAME_PARITY_CORE = (None, 1, 4, 4, 4, 5, 5, 5)
+CABLE_CORE = (0, 0, 1, 1, 4, 4, 5, 5)
 
 
 def relay_of(src, dst):
@@ -21,7 +22,7 @@ def relay_of(src, dst):
     if hs == hd:
         return hs * 128 + c * 8 + (SAME_PARITY_CORE[t] if same_parity else MATE_PORT_CORE[t])
     if same_parity:
-        return (hs ^ 1) * 128 + cd * 8 + t
+        return (hs ^ 1) * 128 + cd * 8 + CABLE_CORE[t]
     return (3 - hs) * 128 + c * 8 + MATE_PORT_CORE[t]
 
 

import comms_topo
from concourse.bass import DstId, RemoteDMATransfer

B = 16

SCRATCH = {
    "send": ("sbuf", [128, 512], "float32"),
    "land": ("sbuf", [128, 512], "float32"),
}
SEMAPHORES = ["loaded", "kept", "read", "arrived", "stored"]

MATE_PORT_CORE = (6, 6, 7, 7, 2, 2, 3, 3)
SAME_PARITY_CORE = (None, 1, 4, 4, 4, 5, 5, 5)
CABLE_CORE = (0, 0, 1, 1, 4, 4, 5, 5)


def relay_of(src, dst):
    hs, hd = comms_topo.host(src), comms_topo.host(dst)
    c, cd = comms_topo.chip(src), comms_topo.chip(dst)
    t = (cd // 2 - c // 2) % 8
    same_parity = c % 2 == cd % 2
    if hs == hd:
        return hs * 128 + c * 8 + (SAME_PARITY_CORE[t] if same_parity else MATE_PORT_CORE[t])
    if same_parity:
        return (hs ^ 1) * 128 + cd * 8 + CABLE_CORE[t]
    return (3 - hs) * 128 + c * 8 + MATE_PORT_CORE[t]


def jobs_of(relay, cores):
    return [(i, j) for i, s in enumerate(cores) for j, d in enumerate(cores) if s != d and relay_of(s, d) == relay]


def engines_each(n):
    return {1: 8, 2: 4, 3: 2}[n]


def block(t, k):
    return t[:, k * B:(k + 1) * B]


def transfer(T, src_core, dst_core, src_ap, dst_ap, mask):
    rid, pid = comms_topo.addr(dst_core, src_core)
    return RemoteDMATransfer(dst_ids=[DstId(rid=rid, pnc=pid)], dma_engine_mask=mask, remote_sem=T.sem.arrived,
                             src=src_ap, dst=dst_ap)


def rank_program(g, core, T, topo):
    cores = list(T.cores)
    rank = T.rank_of(core)

    if rank is None:
        jobs = jobs_of(core, cores)
        if not jobs:
            return
        e = engines_each(len(jobs))
        g.wait_ge(T.sem.arrived, len(jobs))
        g.remote_dma_fused(
            [transfer(T, core, cores[j], block(T.land, slot), block(T.land, i), ((1 << e) - 1) << (slot * e))
             for slot, (i, j) in enumerate(jobs)],
            local_sem=T.sem.read)
        g.wait_ge(T.sem.read, e * len(jobs))
        return

    g.dma_start(T.send[:], T.x[:]).then_inc(T.sem.loaded, 16)
    g.dma_start(block(T.land, rank), block(T.x, rank)).then_inc(T.sem.kept, 16)

    off_chip, on_chip, expected = [], [], 0
    for j, d in enumerate(cores):
        if d == core:
            continue
        out_relay = relay_of(core, d)
        slot = jobs_of(out_relay, cores).index((rank, j))
        (on_chip if out_relay // 8 == core // 8 else off_chip).append((out_relay, j, slot))
        expected += engines_each(len(jobs_of(relay_of(d, core), cores)))
    off_chip.sort(key=lambda w: comms_topo.rack(comms_topo.host(w[0])) == comms_topo.rack(comms_topo.host(core)))

    g.wait_ge(T.sem.loaded, 16)
    for k in range(2):
        g.remote_dma_fused(
            [transfer(T, core, r, block(T.send, j), block(T.land, slot), 1 << n)
             for n, (r, j, slot) in enumerate(off_chip[8 * k:8 * k + 8])] +
            [transfer(T, core, r, block(T.send, j), block(T.land, slot), 1 << (8 + n))
             for n, (r, j, slot) in enumerate(on_chip[8 * k:8 * k + 8])],
            local_sem=T.sem.read)

    g.wait_ge(T.sem.arrived, expected)
    g.wait_ge(T.sem.kept, 16)
    g.dma_start(T.y[:], T.land[:]).then_inc(T.sem.stored, 16)
    g.wait_ge(T.sem.read, len(off_chip) + len(on_chip))
    g.wait_ge(T.sem.stored, 16)
